import numpy as np
import ml_dtypes


def mxq(x, axis, fmt="e4m3"):
    dtype, down = {"e4m3": (ml_dtypes.float8_e4m3fn, 7), "e5m2": (ml_dtypes.float8_e5m2, 14)}[fmt]
    v = np.moveaxis(np.asarray(x, np.float32).astype(ml_dtypes.bfloat16).astype(np.float64), axis, -1)
    blocks = v.reshape(v.shape[:-1] + (-1, 32))
    amax = np.abs(blocks).max(-1, keepdims=True)
    byte = np.maximum(np.where(amax > 0, np.frexp(amax)[1] - 1 + 127, 0) - down, 1)
    scale = np.exp2(byte - 127.0)
    codes = (blocks / scale).astype(np.float32).astype(dtype).astype(np.float64)
    return np.moveaxis((codes * scale).reshape(v.shape), -1, axis)


WIDE = False


def mx_kscale(k):
    if not WIDE:
        return np.ones(k)
    levels = np.array([10, -10, 5, -5, 0])
    if k % 512:
        return np.exp2(np.random.permutation(np.resize(levels, k // 32))).repeat(32)
    a = np.empty((k // 512, 16))
    for p in range(k // 512):
        a[p, :8] = np.random.permutation(np.resize(levels, 8))
        for g in range(8):
            far = levels[np.abs(levels - a[p, g]) >= 10]
            a[p, g + 8] = far[np.random.randint(len(far))]
    return np.exp2(a.ravel()).repeat(32)


def f64(x):
    return np.asarray(x).astype(np.float64)


def striped(idx):
    return np.tile(idx.reshape(-1, 16).T, (8, 1)).astype(np.uint16)


def unstriped(offs):
    return offs[:16].T.reshape(-1).astype(np.int64)


def pack_weight(w):
    k, n = w.shape
    w = f64(np.asarray(w, np.float32).astype(ml_dtypes.bfloat16)).reshape(k // 32, 32, n)
    amax = np.abs(w).max(1)
    byte = np.clip(np.where(amax > 0, np.frexp(amax)[1] - 1 + 127 - 7, 1), 1, 254)
    scaled = (w * np.exp2(127.0 - byte)[:, None, :]).reshape(k, n).astype(np.float32)
    words = np.ascontiguousarray(scaled.reshape(k // 512, 128, 4, n).transpose(0, 1, 3, 2)).astype(ml_dtypes.float8_e4m3fn).view(np.uint8)
    return words, np.ascontiguousarray(byte.astype(np.uint8).reshape(k // 512, 16, n))


def unpack_weight(words, scales):
    g, p, n, _ = words.shape
    vals = np.ascontiguousarray(words).view(ml_dtypes.float8_e4m3fn).astype(np.float64) * np.repeat(np.exp2(scales.astype(np.float64) - 127.0), 8, axis=1)[..., None]
    return vals.transpose(0, 1, 3, 2).reshape(g * 512, n)


E2M1 = np.array([0.0, 0.5, 1.0, 1.5, 2.0, 3.0, 4.0, 6.0, -0.0, -0.5, -1.0, -1.5, -2.0, -3.0, -4.0, -6.0])


def pack_fp4(w):
    k, n = w.shape
    w = f64(np.asarray(w, np.float32).astype(ml_dtypes.bfloat16)).reshape(k // 32, 32, n)
    amax = np.abs(w).max(1)
    mant, ex = np.frexp(amax / 6.0)
    byte = np.clip(np.where(amax > 0, np.where(mant > 0.5, ex, ex - 1) + 127, 1), 1, 254)
    scaled = (w * np.exp2(127.0 - byte)[:, None, :]).reshape(k, n).astype(np.float32)
    c = np.ascontiguousarray(scaled.reshape(k // 512, 128, 4, n).transpose(0, 1, 3, 2)).astype(ml_dtypes.float4_e2m1fn).view(np.uint8) & 0xF
    words = (c[..., 0::2] | (c[..., 1::2] << 4)).reshape(k // 512, 128, 2 * n)
    return np.ascontiguousarray(words), np.ascontiguousarray(byte.astype(np.uint8).reshape(k // 512, 16, n))


def unpack_fp4(words, scales):
    g, _, n = scales.shape
    words = np.ascontiguousarray(words).reshape(g, 128, n, 2)
    nib = np.empty((g, 128, n, 4), np.uint8)
    nib[..., 0::2] = words & 0xF
    nib[..., 1::2] = words >> 4
    vals = E2M1[nib] * np.repeat(np.exp2(scales.astype(np.float64) - 127.0), 8, axis=1)[..., None]
    return vals.transpose(0, 1, 3, 2).reshape(g * 512, n)


def relu(v):
    return np.maximum(v, 0.0)


K, T, S, D, N, H = 512, 2048, 1024, 2, 128, 512


def setup_inputs():
    n = np.random.standard_normal
    s = mx_kscale(K)[:, None]
    u = mx_kscale(H)
    packed_xT = pack_weight(n((K, T)) * s)
    packed_w1 = pack_fp4(n((K, H)) / np.sqrt(K) / s)
    packed_w2 = pack_fp4(n((K, H)) / np.sqrt(K) / s)
    packed_w3 = pack_fp4(n((H, N)) / np.sqrt(H) / u[:, None])
    return {
        "x_words": packed_xT[0],
        "x_scales": packed_xT[1],
        "w1_words": packed_w1[0],
        "w1_scales": packed_w1[1],
        "w2_words": packed_w2[0],
        "w2_scales": packed_w2[1],
        "infl": (np.random.uniform(0.5, 2.0, (H, S))).astype(np.float32),
        "unit": (np.random.uniform(0.6, 1.4, (H, 1)) * u[:, None]).astype(np.float32),
        "w3_words": packed_w3[0],
        "w3_scales": packed_w3[1],
        "offs": striped(np.random.permutation(T)[:S]),
        "shr": striped(np.random.permutation(S)),
    }


def reference(x_words, x_scales, w1_words, w1_scales, w2_words, w2_scales, infl, unit, w3_words, w3_scales, offs, shr):
    xq = unpack_weight(x_words, x_scales)[:, unstriped(offs)]
    bw = unpack_fp4(w1_words, w1_scales).T @ xq
    btl = np.log(np.exp(bw) + 1.0)
    rt = unpack_fp4(w2_words, w2_scales).T @ xq
    rtt = np.log(np.exp(rt) + 1.0) + 0.3
    bdp = btl * rtt
    que = relu(f64(infl) - (0.7 * bdp))
    qs = que[:, unstriped(shr)]
    bs = btl[:, unstriped(shr)]
    pace = (btl * (qs + 0.5)) / (que + bs + 0.5)
    pairsum = np.repeat(pace.reshape(len(pace), -1, D).sum(axis=2), D, axis=1)
    hid = f64(unit) * ((pace / pairsum) * rtt)
    return unpack_fp4(w3_words, w3_scales).T @ mxq(hid, 0, "e4m3")

@@ -1,0 +1,250 @@
+from contextlib import ExitStack
+
+import concourse.mybir as mybir
+
+F32 = mybir.dt.float32
+BF16 = mybir.dt.bfloat16
+I32 = mybir.dt.int32
+U32 = mybir.dt.uint32
+U16 = mybir.dt.uint16
+U8 = mybir.dt.uint8
+FP8X4 = mybir.dt.float8_e4m3fn_x4
+FP4X4 = mybir.dt.float4_e2m1fn_x4
+ACT = mybir.ActivationFunctionType
+ALU = mybir.AluOpType
+
+K, T, S, H, N = 512, 2048, 1024, 512, 128
+FLOPS = 2 * K * H * S * 2 + 2 * H * N * S
+P = 128
+PACK = 4
+BANK = 512
+TINY = 2.0 ** -60
+WORD_PIECES = ((0, 256), (256, 512), (512, 768), (768, 1024))
+OUT_PIECES = ((0, 256), (256, 512), (512, 768), (768, 896), (896, 1024))
+FUSED = [1]
+
+
+def tile_picked_ytcpcc_shr_p_kernel(tc, x_words, x_scales, w1_words, w1_scales, w2_words, w2_scales, infl, unit, w3_words, w3_scales, offs, shr, out):
+    nc = tc.nc
+    with ExitStack() as ctx:
+        keep = ctx.enter_context(tc.tile_pool(name="keep", bufs=1))
+        psum = ctx.enter_context(tc.psum_pool(name="psum", bufs=1))
+
+        def load_scales(queues, plane, rows):
+            for r in range(4):
+                queues[r % len(queues)].dma_start(out=plane[r:P:32, :].bitcast(I32), in_=rows[0][r:16:4, :].bitcast(I32))
+
+        offs_sb = keep.tile([P, S // 16], U16, name="offs_sb")
+        shr_sb = keep.tile([P, S // 16], U16, name="shr_sb")
+        xw = keep.tile([P, T], U32, name="xw", align_bytes=64)
+        xs = keep.tile([P, T], U8, name="xs", align_bytes=64)
+        ww = [keep.tile([P, 2 * H], U8, name=f"ww{a}", tag=f"raw{a}", align_bytes=64) for a in range(2)]
+        ws = [keep.tile([P, H], U8, name=f"ws{a}", tag=f"raw{2 + a}", align_bytes=64) for a in range(2)]
+
+        nc.vector.memset(xs[:].bitcast(I32), 0)
+        nc.vector.memset(ws[0][:].bitcast(I32), 0)
+        nc.vector.memset(ws[1][:].bitcast(I32), 0)
+
+        both = (nc.sync, nc.scalar)
+        nc.sync.dma_start(out=offs_sb[:], in_=offs)
+        nc.scalar.dma_start(out=ww[0][:].bitcast(I32), in_=w1_words[0].bitcast(I32))
+        load_scales(both, xs, x_scales)
+        nc.sync.dma_start(out=xw[:].bitcast(I32), in_=x_words[0].rearrange("p n t -> p (n t)").bitcast(I32))
+        nc.scalar.dma_start(out=ww[1][:].bitcast(I32), in_=w2_words[0].bitcast(I32))
+        load_scales(both, ws[0], w1_scales)
+        load_scales(both, ws[1], w2_scales)
+        nc.sync.dma_start(out=shr_sb[:], in_=shr)
+
+        dw = [[keep.tile([P, 2, 2 * P], U8, name=f"dw{a}_{g}", tag=f"dw{a}_{g}", align_bytes=64) for g in range(2)] for a in range(2)]
+        ds = [[keep.tile([P, 2, P], U8, name=f"ds{a}_{g}", tag=f"ds{a}_{g}", align_bytes=64) for g in range(2)] for a in range(2)]
+
+        def deal_words(a, g):
+            nc.vector.tensor_copy(out=dw[a][g][:].rearrange("p t (m b) -> p t m b", b=2),
+                                  in_=ww[a][:].rearrange("p (m t b) -> p t m b", t=PACK, b=2)[:, 2 * g : 2 * g + 2])
+
+        def deal_scales(a, g):
+            nc.vector.tensor_copy(out=ds[a][g][:], in_=ws[a][:].rearrange("p (m t) -> p t m", t=PACK)[:, 2 * g : 2 * g + 2])
+
+        gw = [keep.tile([P, b - a], U32, name=f"gw{a}", align_bytes=64) for a, b in WORD_PIECES]
+        gs = [keep.tile([P, BANK], U8, name=f"gs{h}", align_bytes=64) for h in range(2)]
+
+        def pick_scales(h):
+            nc.vector.tensor_copy(out=gs[h][:], in_=xs[:].indirect(offs_sb[:, h * BANK // 16 : (h + 1) * BANK // 16]))
+
+        def pick_words(k):
+            a, b = WORD_PIECES[k]
+            nc.vector.tensor_copy(out=gw[k][:], in_=xw[:].indirect(offs_sb[:, a // 16 : b // 16]))
+
+        sg = {}
+        ln = {}
+        btl = [keep.tile([P, S], F32, name=f"btl{t}") for t in range(PACK)]
+        bdp = [keep.tile([P, S], F32, name=f"bdp{t}") for t in range(PACK)]
+        qs = [keep.tile([P, S], F32, name=f"qs{t}") for t in range(PACK)]
+        den = [keep.tile([P, S], F32, name=f"den{t}") for t in range(PACK)]
+        que5 = {t: keep.tile([P, S], F32, name=f"que5_{t}") for t in FUSED}
+        pair = [keep.tile([P, S // 2], F32, name=f"pair{t}") for t in range(PACK)]
+        lnp = keep.tile([P, PACK, S // 2], F32, name="lnp")
+        top = keep.tile([P, PACK, S], F32, name="top")
+        banks = {}
+
+        def open_banks(t, slot):
+            for a in range(2):
+                sg[a, t] = keep.tile([P, S], F32, name=f"sg{a}_{t}", tag=f"sg{a}_{t}")
+                for h in range(2):
+                    banks[t, a, h] = psum.tile([P, BANK], F32, name=f"acc{t}_{a}_{h}", tag=f"bank{slot}_{a}_{h}")
+
+        def product(t, a, k):
+            lo, hi = WORD_PIECES[k]
+            h = lo // BANK
+            cols = slice(lo - h * BANK, hi - h * BANK)
+            nc.tensor.matmul_mx(out=banks[t, a, h][:, cols], lhsT=dw[a][t // 2][:, t % 2, :].bitcast(FP4X4),
+                                lhsT_scale=ds[a][t // 2][:, t % 2, :],
+                                rhs=gw[k][:].bitcast(FP8X4), rhs_scale=gs[h][:, cols], start=True, stop=True)
+
+        def sigmoid(t, a, lo, hi):
+            h = lo // BANK
+            nc.scalar.activation(out=sg[a, t][:, lo:hi], in_=banks[t, a, h][:, lo - h * BANK : hi - h * BANK],
+                                 func=ACT.Sigmoid, scale=-1.0)
+
+        def logs(order):
+            for a, t in order:
+                ln[a, t] = sg[a, t]
+                nc.scalar.activation(out=ln[a, t][:], in_=sg[a, t][:], func=ACT.Ln, bias=TINY)
+
+        def softplus(t):
+            for a, dst in ((1, ln[1, t]), (0, btl[t])):
+                for h in range(2):
+                    cols = slice(h * BANK, (h + 1) * BANK)
+                    nc.vector.scalar_tensor_tensor(out=dst[:, cols], in0=ln[a, t][:, cols], scalar=-1.0,
+                                                   in1=banks[t, a, h][:], op0=ALU.mult, op1=ALU.max)
+
+        def queue(t):
+            nc.vector.scalar_tensor_tensor(out=bdp[t][:], in0=ln[1, t][:], scalar=0.3, in1=btl[t][:], op0=ALU.add, op1=ALU.mult)
+            nc.vector.scalar_tensor_tensor(out=q[t][:], in0=bdp[t][:], scalar=-0.7, in1=q[t][:], op0=ALU.mult, op1=ALU.add)
+
+        def share(dst, src, bias):
+            for h in range(2):
+                nc.scalar.activation(out=dst[:, h * BANK : (h + 1) * BANK],
+                                     in_=src[:].indirect(shr_sb[:, h * BANK // 16 : (h + 1) * BANK // 16]),
+                                     func=ACT.Copy, bias=bias)
+
+        def share_b(t):
+            if t not in FUSED:
+                share(den[t], btl[t], 0.5)
+
+        def share_q(t):
+            share(qs[t], q[t], 0.5)
+
+        def denominator(t):
+            if t in FUSED:
+                nc.vector.tensor_scalar(out=que5[t][:], in0=q[t][:], scalar1=0.0, scalar2=0.5, op0=ALU.max, op1=ALU.add)
+                for h in range(2):
+                    cols = slice(h * BANK, (h + 1) * BANK)
+                    nc.vector.tensor_tensor(out=den[t][:, cols], in0=btl[t][:].indirect(shr_sb[:, h * BANK // 16 : (h + 1) * BANK // 16]),
+                                            in1=que5[t][:, cols], op=ALU.add)
+            else:
+                nc.vector.scalar_tensor_tensor(out=den[t][:], in0=q[t][:], scalar=0.0, in1=den[t][:], op0=ALU.max, op1=ALU.add)
+
+        def pairs(t):
+            swapped = den[t][:].rearrange("p (v d) -> p v d", d=2)[:, :, ::-1]
+            qs3 = qs[t][:].rearrange("p (v d) -> p v d", d=2)
+            nc.vector.scalar_tensor_tensor(out=qs3, in0=qs3, scalar=0.5, in1=swapped, op0=ALU.max, op1=ALU.mult)
+            nc.vector.tensor_tensor(out=den[t][:], in0=btl[t][:], in1=qs[t][:], op=ALU.mult)
+            c3 = den[t][:].rearrange("p (v d) -> p v d", d=2)
+            nc.vector.tensor_tensor(out=pair[t][:], in0=c3[:, :, 0], in1=c3[:, :, 1], op=ALU.add)
+
+        def log_pair(t):
+            nc.scalar.activation(out=lnp[:, t, :], in_=pair[t][:], func=ACT.Ln)
+
+        def numerator(t):
+            nc.vector.scalar_tensor_tensor(out=top[:, t, :], in0=bdp[t][:], scalar=unit_sb[:, t : t + 1], in1=qs[t][:],
+                                           op0=ALU.mult, op1=ALU.mult)
+
+        def finish(k):
+            lo, hi = OUT_PIECES[k]
+            n = hi - lo
+            rec = keep.tile([P, n // 4, PACK, 2], F32, name=f"rec{k}")
+            nc.scalar.activation(out=rec[:], in_=lnp[:, :, lo // 2 : hi // 2].rearrange("p t (c v) -> p c t v", v=2),
+                                 func=ACT.Exp, scale=-1.0)
+            hid = keep.tile([P, n * PACK], BF16, name=f"hid{k}", align_bytes=64)
+            nc.vector.tensor_tensor(out=hid[:].rearrange("p (c v d t) -> p c t v d", v=2, d=2, t=PACK),
+                                    in0=top[:, :, lo:hi].rearrange("p t (c v d) -> p c t v d", v=2, d=2),
+                                    in1=rec[:].unsqueeze(4).to_broadcast([P, n // 4, PACK, 2, 2]), op=ALU.mult)
+            codes = keep.tile([P, n], U32, name=f"codes{k}", align_bytes=64)
+            scales = keep.tile([P, n], U8, name=f"scales{k}", align_bytes=64)
+            nc.vector.quantize_mx(out=codes[:].bitcast(FP8X4), scales=scales[:], in_=hid[:])
+            acc = psum.tile([P, n], F32, name=f"res{k}", tag=f"bank{k // 4}_{k // 2 % 2}_{k % 2}")
+            nc.tensor.matmul_mx(out=acc[:], lhsT=w3w[:].bitcast(FP4X4), lhsT_scale=w3s[:],
+                                rhs=codes[:].bitcast(FP8X4), rhs_scale=scales[:], start=True, stop=True)
+            res = keep.tile([P, n], F32, name=f"out{k}")
+            nc.scalar.copy(out=res[:], in_=acc[:])
+            nc.sync.dma_start(out=out[:, lo:hi], in_=res[:])
+
+        open_banks(0, 0)
+        open_banks(1, 1)
+        deal_words(0, 0)
+        pick_scales(0)
+        deal_words(1, 0)
+        deal_scales(0, 0)
+        deal_scales(1, 0)
+        for k in range(len(WORD_PIECES)):
+            if k == 2:
+                pick_scales(1)
+            pick_words(k)
+            for t in (1, 0):
+                for a in range(2):
+                    product(t, a, k)
+            for t in (1, 0):
+                for a in range(2):
+                    sigmoid(t, a, *WORD_PIECES[k])
+        for a in range(2):
+            deal_words(a, 1)
+            deal_scales(a, 1)
+        infl_rows = infl.rearrange("(p t) j -> p t j", t=PACK)
+        q = [keep.tile([P, S], F32, name=f"q{t}", tag=f"raw{t}", align_bytes=64) for t in range(PACK)]
+        for t in range(PACK):
+            nc.sync.dma_start(out=q[t][:], in_=infl_rows[:, t, :])
+        unit_sb = keep.tile([P, PACK], F32, name="unit_sb", tag="ds0_0", align_bytes=64)
+        w3w = keep.tile([P, 2 * N], U8, name="w3w", tag="dw0_0", align_bytes=64)
+        w3s = keep.tile([P, N], U8, name="w3s", tag="dw1_0", align_bytes=64)
+        nc.sync.dma_start(out=unit_sb[:], in_=unit.rearrange("(p t) o -> p (t o)", t=PACK))
+        nc.sync.dma_start(out=w3w[:].bitcast(I32), in_=w3_words[0].bitcast(I32))
+        nc.vector.memset(w3s[:].bitcast(I32), 0)
+        load_scales((nc.sync,), w3s, w3_scales)
+
+        logs(((1, 0), (0, 0), (1, 1), (0, 1)))
+        for t in (0, 1):
+            softplus(t)
+            queue(t)
+        share_b(0)
+        share_q(0)
+        for t, slot in ((3, 0), (2, 1)):
+            open_banks(t, slot)
+            for a in range(2):
+                for k in range(len(WORD_PIECES)):
+                    product(t, a, k)
+                for h in range(2):
+                    sigmoid(t, a, h * BANK, (h + 1) * BANK)
+        logs(((1, 2), (0, 2), (1, 3), (0, 3)))
+        denominator(0)
+        pairs(0)
+        share_b(1)
+        share_q(1)
+        denominator(1)
+        for t in (2, 3):
+            softplus(t)
+            queue(t)
+        for t in (2, 3):
+            share_b(t)
+            share_q(t)
+
+        pairs(1)
+        for t in (2, 3):
+            denominator(t)
+            pairs(t)
+        for t in range(PACK):
+            log_pair(t)
+        for t in range(PACK):
+            numerator(t)
+        for k in range(len(OUT_PIECES)):
+            finish(k)

@@ -17,162 +17,172 @@ K, T, S, H, N = 512, 2048, 1024, 512, 128
 FLOPS = 2 * K * H * S * 2 + 2 * H * N * S
 P = 128
 PACK = 4
-BANK = 512
+HALF = 512
 TINY = 2.0 ** -60
-WORD_PIECES = ((0, 256), (256, 512), (512, 768), (768, 1024))
 OUT_PIECES = ((0, 256), (256, 512), (512, 768), (768, 896), (896, 1024))
-FUSED = [1]
+FUSED_TILE = 1
 
 
 def tile_picked_ytcpcc_shr_p_kernel(tc, x_words, x_scales, w1_words, w1_scales, w2_words, w2_scales, infl, unit, w3_words, w3_scales, offs, shr, out):
     nc = tc.nc
+    halves = [slice(h * HALF, (h + 1) * HALF) for h in range(2)]
+    list_halves = [slice(h * HALF // 16, (h + 1) * HALF // 16) for h in range(2)]
     with ExitStack() as ctx:
         keep = ctx.enter_context(tc.tile_pool(name="keep", bufs=1))
         psum = ctx.enter_context(tc.psum_pool(name="psum", bufs=1))
 
-        def load_scales(queues, plane, rows):
-            for r in range(4):
-                queues[r % len(queues)].dma_start(out=plane[r:P:32, :].bitcast(I32), in_=rows[0][r:16:4, :].bitcast(I32))
+        def load_scale_rows(queue, plane, rows, r):
+            queue.dma_start(out=plane[r:P:32, :].bitcast(I32), in_=rows[0][r:16:4, :].bitcast(I32))
 
         offs_sb = keep.tile([P, S // 16], U16, name="offs_sb")
         shr_sb = keep.tile([P, S // 16], U16, name="shr_sb")
-        xw = keep.tile([P, T], U32, name="xw", align_bytes=64)
+        xw = keep.tile([P, T], U32, name="xw", tag="xw", align_bytes=64)
         xs = keep.tile([P, T], U8, name="xs", align_bytes=64)
         ww = [keep.tile([P, 2 * H], U8, name=f"ww{a}", tag=f"raw{a}", align_bytes=64) for a in range(2)]
         ws = [keep.tile([P, H], U8, name=f"ws{a}", tag=f"raw{2 + a}", align_bytes=64) for a in range(2)]
 
         nc.vector.memset(xs[:].bitcast(I32), 0)
-        nc.vector.memset(ws[0][:].bitcast(I32), 0)
-        nc.vector.memset(ws[1][:].bitcast(I32), 0)
+        nc.gpsimd.memset(ws[0][:].bitcast(I32), 0)
+        nc.gpsimd.memset(ws[1][:].bitcast(I32), 0)
 
         both = (nc.sync, nc.scalar)
         nc.sync.dma_start(out=offs_sb[:], in_=offs)
         nc.scalar.dma_start(out=ww[0][:].bitcast(I32), in_=w1_words[0].bitcast(I32))
-        load_scales(both, xs, x_scales)
-        nc.sync.dma_start(out=xw[:].bitcast(I32), in_=x_words[0].rearrange("p n t -> p (n t)").bitcast(I32))
+        for r in range(4):
+            load_scale_rows(both[r % 2], xs, x_scales, r)
+        load_scale_rows(nc.sync, ws[0], w1_scales, 0)
+        nc.scalar.dma_start(out=xw[:].bitcast(I32), in_=x_words[0].rearrange("p n t -> p (n t)").bitcast(I32))
+        for r in range(1, 4):
+            load_scale_rows(both[(r + 1) % 2], ws[0], w1_scales, r)
         nc.scalar.dma_start(out=ww[1][:].bitcast(I32), in_=w2_words[0].bitcast(I32))
-        load_scales(both, ws[0], w1_scales)
-        load_scales(both, ws[1], w2_scales)
+        for r in range(4):
+            load_scale_rows(nc.scalar if r == 1 else nc.sync, ws[1], w2_scales, r)
         nc.sync.dma_start(out=shr_sb[:], in_=shr)
 
-        dw = [[keep.tile([P, 2, 2 * P], U8, name=f"dw{a}_{g}", tag=f"dw{a}_{g}", align_bytes=64) for g in range(2)] for a in range(2)]
-        ds = [[keep.tile([P, 2, P], U8, name=f"ds{a}_{g}", tag=f"ds{a}_{g}", align_bytes=64) for g in range(2)] for a in range(2)]
+        dw = {}
+        ds = {}
 
-        def deal_words(a, g):
-            nc.vector.tensor_copy(out=dw[a][g][:].rearrange("p t (m b) -> p t m b", b=2),
-                                  in_=ww[a][:].rearrange("p (m t b) -> p t m b", t=PACK, b=2)[:, 2 * g : 2 * g + 2])
+        def deal_words(engine, a, g):
+            engine.tensor_copy(out=dw[a, g].rearrange("p (t m b) -> p t m b", t=2, b=2),
+                               in_=ww[a][:].rearrange("p (m t b) -> p t m b", t=PACK, b=2)[:, 2 * g : 2 * g + 2])
 
-        def deal_scales(a, g):
-            nc.vector.tensor_copy(out=ds[a][g][:], in_=ws[a][:].rearrange("p (m t) -> p t m", t=PACK)[:, 2 * g : 2 * g + 2])
+        def deal_scales(engine, a, g):
+            engine.tensor_copy(out=ds[a, g].rearrange("p (t m) -> p t m", t=2),
+                               in_=ws[a][:].rearrange("p (m t) -> p t m", t=PACK)[:, 2 * g : 2 * g + 2])
 
-        gw = [keep.tile([P, b - a], U32, name=f"gw{a}", align_bytes=64) for a, b in WORD_PIECES]
-        gs = [keep.tile([P, BANK], U8, name=f"gs{h}", align_bytes=64) for h in range(2)]
+        for a in range(2):
+            dw[a, 0] = keep.tile([P, 4 * P], U8, name=f"dw{a}", tag=f"dw{a}", align_bytes=64)[:]
+            ds[a, 0] = keep.tile([P, 2 * P], U8, name=f"ds{a}", tag=f"ds{a}", align_bytes=64)[:]
+
+        gw = [keep.tile([P, HALF], U32, name=f"gw{h}", align_bytes=64) for h in range(2)]
+        gs = [keep.tile([P, HALF], U8, name=f"gs{h}", align_bytes=64) for h in range(2)]
 
         def pick_scales(h):
-            nc.vector.tensor_copy(out=gs[h][:], in_=xs[:].indirect(offs_sb[:, h * BANK // 16 : (h + 1) * BANK // 16]))
+            nc.vector.tensor_copy(out=gs[h][:], in_=xs[:].indirect(offs_sb[:, list_halves[h]]))
 
-        def pick_words(k):
-            a, b = WORD_PIECES[k]
-            nc.vector.tensor_copy(out=gw[k][:], in_=xw[:].indirect(offs_sb[:, a // 16 : b // 16]))
+        def pick_words(h):
+            nc.vector.tensor_copy(out=gw[h][:], in_=xw[:].indirect(offs_sb[:, list_halves[h]]))
 
-        sg = {}
-        ln = {}
+        sg = [keep.tile([P, 2, S], F32, name=f"sg{t}") for t in range(PACK)]
         btl = [keep.tile([P, S], F32, name=f"btl{t}") for t in range(PACK)]
         bdp = [keep.tile([P, S], F32, name=f"bdp{t}") for t in range(PACK)]
         qs = [keep.tile([P, S], F32, name=f"qs{t}") for t in range(PACK)]
         den = [keep.tile([P, S], F32, name=f"den{t}") for t in range(PACK)]
-        que5 = {t: keep.tile([P, S], F32, name=f"que5_{t}") for t in FUSED}
+        que5 = keep.tile([P, S], F32, name="que5")
         pair = [keep.tile([P, S // 2], F32, name=f"pair{t}") for t in range(PACK)]
         lnp = keep.tile([P, PACK, S // 2], F32, name="lnp")
         top = keep.tile([P, PACK, S], F32, name="top")
         banks = {}
 
-        def open_banks(t, slot):
-            for a in range(2):
-                sg[a, t] = keep.tile([P, S], F32, name=f"sg{a}_{t}", tag=f"sg{a}_{t}")
-                for h in range(2):
-                    banks[t, a, h] = psum.tile([P, BANK], F32, name=f"acc{t}_{a}_{h}", tag=f"bank{slot}_{a}_{h}")
+        def product(t, a, h, slot):
+            banks[t, a, h] = psum.tile([P, HALF], F32, name=f"acc{t}_{a}_{h}", tag=f"bank{slot}_{a}_{h}")
+            g, i = divmod(t, 2)
+            nc.tensor.matmul_mx(out=banks[t, a, h][:], lhsT=dw[a, g][:, 2 * P * i : 2 * P * (i + 1)].bitcast(FP4X4),
+                                lhsT_scale=ds[a, g][:, P * i : P * (i + 1)],
+                                rhs=gw[h][:].bitcast(FP8X4), rhs_scale=gs[h][:], start=True, stop=True)
 
-        def product(t, a, k):
-            lo, hi = WORD_PIECES[k]
-            h = lo // BANK
-            cols = slice(lo - h * BANK, hi - h * BANK)
-            nc.tensor.matmul_mx(out=banks[t, a, h][:, cols], lhsT=dw[a][t // 2][:, t % 2, :].bitcast(FP4X4),
-                                lhsT_scale=ds[a][t // 2][:, t % 2, :],
-                                rhs=gw[k][:].bitcast(FP8X4), rhs_scale=gs[h][:, cols], start=True, stop=True)
+        def sigmoid(t, a, h):
+            nc.scalar.activation(out=sg[t][:, a, halves[h]], in_=banks[t, a, h][:], func=ACT.Sigmoid, scale=-1.0)
 
-        def sigmoid(t, a, lo, hi):
-            h = lo // BANK
-            nc.scalar.activation(out=sg[a, t][:, lo:hi], in_=banks[t, a, h][:, lo - h * BANK : hi - h * BANK],
-                                 func=ACT.Sigmoid, scale=-1.0)
-
-        def logs(order):
-            for a, t in order:
-                ln[a, t] = sg[a, t]
-                nc.scalar.activation(out=ln[a, t][:], in_=sg[a, t][:], func=ACT.Ln, bias=TINY)
+        def logs(t):
+            for h in range(2):
+                nc.scalar.activation(out=sg[t][:, :, halves[h]], in_=sg[t][:, :, halves[h]], func=ACT.Ln, bias=TINY)
 
         def softplus(t):
-            for a, dst in ((1, ln[1, t]), (0, btl[t])):
-                for h in range(2):
-                    cols = slice(h * BANK, (h + 1) * BANK)
-                    nc.vector.scalar_tensor_tensor(out=dst[:, cols], in0=ln[a, t][:, cols], scalar=-1.0,
+            for h in range(2):
+                for a, dst in ((1, sg[t][:, 1, halves[h]]), (0, btl[t][:, halves[h]])):
+                    nc.vector.scalar_tensor_tensor(out=dst, in0=sg[t][:, a, halves[h]], scalar=-1.0,
                                                    in1=banks[t, a, h][:], op0=ALU.mult, op1=ALU.max)
 
         def queue(t):
-            nc.vector.scalar_tensor_tensor(out=bdp[t][:], in0=ln[1, t][:], scalar=0.3, in1=btl[t][:], op0=ALU.add, op1=ALU.mult)
-            nc.vector.scalar_tensor_tensor(out=q[t][:], in0=bdp[t][:], scalar=-0.7, in1=q[t][:], op0=ALU.mult, op1=ALU.add)
+            for c in halves:
+                nc.vector.scalar_tensor_tensor(out=bdp[t][:, c], in0=sg[t][:, 1, c], scalar=0.3, in1=btl[t][:, c],
+                                               op0=ALU.add, op1=ALU.mult)
+            for c in halves:
+                nc.vector.scalar_tensor_tensor(out=q[t][:, c], in0=bdp[t][:, c], scalar=-0.7, in1=q[t][:, c],
+                                               op0=ALU.mult, op1=ALU.add)
 
-        def share(dst, src, bias):
+        def share(dst, src):
             for h in range(2):
-                nc.scalar.activation(out=dst[:, h * BANK : (h + 1) * BANK],
-                                     in_=src[:].indirect(shr_sb[:, h * BANK // 16 : (h + 1) * BANK // 16]),
-                                     func=ACT.Copy, bias=bias)
-
-        def share_b(t):
-            if t not in FUSED:
-                share(den[t], btl[t], 0.5)
-
-        def share_q(t):
-            share(qs[t], q[t], 0.5)
+                nc.scalar.activation(out=dst[:, halves[h]], in_=src[:].indirect(shr_sb[:, list_halves[h]]),
+                                     func=ACT.Copy, bias=0.5)
 
         def denominator(t):
-            if t in FUSED:
-                nc.vector.tensor_scalar(out=que5[t][:], in0=q[t][:], scalar1=0.0, scalar2=0.5, op0=ALU.max, op1=ALU.add)
-                for h in range(2):
-                    cols = slice(h * BANK, (h + 1) * BANK)
-                    nc.vector.tensor_tensor(out=den[t][:, cols], in0=btl[t][:].indirect(shr_sb[:, h * BANK // 16 : (h + 1) * BANK // 16]),
-                                            in1=que5[t][:, cols], op=ALU.add)
-            else:
-                nc.vector.scalar_tensor_tensor(out=den[t][:], in0=q[t][:], scalar=0.0, in1=den[t][:], op0=ALU.max, op1=ALU.add)
+            for c in halves:
+                nc.vector.scalar_tensor_tensor(out=den[t][:, c], in0=q[t][:, c], scalar=0.0, in1=den[t][:, c],
+                                               op0=ALU.max, op1=ALU.add)
 
-        def pairs(t):
-            swapped = den[t][:].rearrange("p (v d) -> p v d", d=2)[:, :, ::-1]
-            qs3 = qs[t][:].rearrange("p (v d) -> p v d", d=2)
-            nc.vector.scalar_tensor_tensor(out=qs3, in0=qs3, scalar=0.5, in1=swapped, op0=ALU.max, op1=ALU.mult)
-            nc.vector.tensor_tensor(out=den[t][:], in0=btl[t][:], in1=qs[t][:], op=ALU.mult)
-            c3 = den[t][:].rearrange("p (v d) -> p v d", d=2)
-            nc.vector.tensor_tensor(out=pair[t][:], in0=c3[:, :, 0], in1=c3[:, :, 1], op=ALU.add)
+        def denominator_fused(t):
+            for c in halves:
+                nc.vector.tensor_scalar(out=que5[:, c], in0=q[t][:, c], scalar1=0.0, scalar2=0.5, op0=ALU.max, op1=ALU.add)
+            for h in range(2):
+                nc.vector.tensor_tensor(out=den[t][:, halves[h]], in0=btl[t][:].indirect(shr_sb[:, list_halves[h]]),
+                                        in1=que5[:, halves[h]], op=ALU.add)
+
+        def by_pairs(ap):
+            return ap.rearrange("p (v d) -> p v d", d=2)
+
+        def cross(t):
+            for c in halves:
+                nc.vector.scalar_tensor_tensor(out=by_pairs(qs[t][:, c]), in0=by_pairs(qs[t][:, c]), scalar=0.5,
+                                               in1=by_pairs(den[t][:, c])[:, :, ::-1], op0=ALU.max, op1=ALU.mult)
+
+        def weigh(t, engine):
+            for c in halves:
+                engine.tensor_tensor(out=den[t][:, c], in0=btl[t][:, c], in1=qs[t][:, c], op=ALU.mult)
+
+        def pair_sum(t):
+            for h in range(2):
+                m = by_pairs(den[t][:, halves[h]])
+                nc.vector.tensor_tensor(out=pair[t][:, h * HALF // 2 : (h + 1) * HALF // 2], in0=m[:, :, 0], in1=m[:, :, 1], op=ALU.add)
 
         def log_pair(t):
             nc.scalar.activation(out=lnp[:, t, :], in_=pair[t][:], func=ACT.Ln)
 
         def numerator(t):
-            nc.vector.scalar_tensor_tensor(out=top[:, t, :], in0=bdp[t][:], scalar=unit_sb[:, t : t + 1], in1=qs[t][:],
-                                           op0=ALU.mult, op1=ALU.mult)
+            for c in halves:
+                nc.vector.scalar_tensor_tensor(out=top[:, t, c], in0=bdp[t][:, c], scalar=unit_sb[:, t : t + 1], in1=qs[t][:, c],
+                                               op0=ALU.mult, op1=ALU.mult)
+
+        hid = {}
+
+        def hidden(k):
+            lo, hi = OUT_PIECES[k]
+            n = hi - lo
+            rec = keep.tile([P, n // 2, PACK], F32, name=f"rec{k}")
+            nc.scalar.activation(out=rec[:], in_=lnp[:, :, lo // 2 : hi // 2].rearrange("p t v -> p v t"),
+                                 func=ACT.Exp, scale=-1.0)
+            hid[k] = keep.tile([P, n * PACK], BF16, name=f"hid{k}", align_bytes=64)
+            nc.vector.tensor_tensor(out=hid[k][:].rearrange("p (v d t) -> p v t d", d=2, t=PACK),
+                                    in0=top[:, :, lo:hi].rearrange("p t (v d) -> p v t d", d=2),
+                                    in1=rec[:].unsqueeze(3).to_broadcast([P, n // 2, PACK, 2]), op=ALU.mult)
 
         def finish(k):
             lo, hi = OUT_PIECES[k]
             n = hi - lo
-            rec = keep.tile([P, n // 4, PACK, 2], F32, name=f"rec{k}")
-            nc.scalar.activation(out=rec[:], in_=lnp[:, :, lo // 2 : hi // 2].rearrange("p t (c v) -> p c t v", v=2),
-                                 func=ACT.Exp, scale=-1.0)
-            hid = keep.tile([P, n * PACK], BF16, name=f"hid{k}", align_bytes=64)
-            nc.vector.tensor_tensor(out=hid[:].rearrange("p (c v d t) -> p c t v d", v=2, d=2, t=PACK),
-                                    in0=top[:, :, lo:hi].rearrange("p t (c v d) -> p c t v d", v=2, d=2),
-                                    in1=rec[:].unsqueeze(4).to_broadcast([P, n // 4, PACK, 2, 2]), op=ALU.mult)
             codes = keep.tile([P, n], U32, name=f"codes{k}", align_bytes=64)
             scales = keep.tile([P, n], U8, name=f"scales{k}", align_bytes=64)
-            nc.vector.quantize_mx(out=codes[:].bitcast(FP8X4), scales=scales[:], in_=hid[:])
+            nc.vector.quantize_mx(out=codes[:].bitcast(FP8X4), scales=scales[:], in_=hid[k][:])
             acc = psum.tile([P, n], F32, name=f"res{k}", tag=f"bank{k // 4}_{k // 2 % 2}_{k % 2}")
             nc.tensor.matmul_mx(out=acc[:], lhsT=w3w[:].bitcast(FP4X4), lhsT_scale=w3s[:],
                                 rhs=codes[:].bitcast(FP8X4), rhs_scale=scales[:], start=True, stop=True)
@@ -180,71 +190,84 @@ def tile_picked_ytcpcc_shr_p_kernel(tc, x_words, x_scales, w1_words, w1_scales, 
             nc.scalar.copy(out=res[:], in_=acc[:])
             nc.sync.dma_start(out=out[:, lo:hi], in_=res[:])
 
-        open_banks(0, 0)
-        open_banks(1, 1)
-        deal_words(0, 0)
+        def first_products(a, h):
+            for t in (1, 0):
+                product(t, a, h, t)
+            for t in (1, 0):
+                sigmoid(t, a, h)
+
+        deal_words(nc.vector, 0, 0)
         pick_scales(0)
-        deal_words(1, 0)
-        deal_scales(0, 0)
-        deal_scales(1, 0)
-        for k in range(len(WORD_PIECES)):
-            if k == 2:
-                pick_scales(1)
-            pick_words(k)
-            for t in (1, 0):
-                for a in range(2):
-                    product(t, a, k)
-            for t in (1, 0):
-                for a in range(2):
-                    sigmoid(t, a, *WORD_PIECES[k])
+        deal_scales(nc.vector, 0, 0)
+        pick_words(0)
+        first_products(0, 0)
+        pick_scales(1)
+        pick_words(1)
+        first_products(0, 1)
+        deal_words(nc.vector, 1, 0)
+        deal_scales(nc.vector, 1, 0)
+        first_products(1, 0)
+        first_products(1, 1)
+
+        late = keep.tile([P, 12 * P], U8, name="late", tag="xw", align_bytes=64)
         for a in range(2):
-            deal_words(a, 1)
-            deal_scales(a, 1)
+            dw[a, 1] = late[:, 6 * P * a : 6 * P * a + 4 * P]
+            ds[a, 1] = late[:, 6 * P * a + 4 * P : 6 * P * (a + 1)]
+            deal_words(nc.gpsimd, a, 1)
+            deal_scales(nc.gpsimd, a, 1)
+
         infl_rows = infl.rearrange("(p t) j -> p t j", t=PACK)
-        q = [keep.tile([P, S], F32, name=f"q{t}", tag=f"raw{t}", align_bytes=64) for t in range(PACK)]
+        q = [keep.tile([P, S], F32, name=f"q{t}", tag=f"raw{(0, 2, 1, 3)[t]}", align_bytes=64) for t in range(PACK)]
         for t in range(PACK):
             nc.sync.dma_start(out=q[t][:], in_=infl_rows[:, t, :])
-        unit_sb = keep.tile([P, PACK], F32, name="unit_sb", tag="ds0_0", align_bytes=64)
-        w3w = keep.tile([P, 2 * N], U8, name="w3w", tag="dw0_0", align_bytes=64)
-        w3s = keep.tile([P, N], U8, name="w3s", tag="dw1_0", align_bytes=64)
+        unit_sb = keep.tile([P, PACK], F32, name="unit_sb", tag="ds0", align_bytes=64)
+        w3w = keep.tile([P, 2 * N], U8, name="w3w", tag="dw0", align_bytes=64)
+        w3s = keep.tile([P, N], U8, name="w3s", tag="dw1", align_bytes=64)
         nc.sync.dma_start(out=unit_sb[:], in_=unit.rearrange("(p t) o -> p (t o)", t=PACK))
         nc.sync.dma_start(out=w3w[:].bitcast(I32), in_=w3_words[0].bitcast(I32))
-        nc.vector.memset(w3s[:].bitcast(I32), 0)
-        load_scales((nc.sync,), w3s, w3_scales)
+        nc.gpsimd.memset(w3s[:].bitcast(I32), 0)
+        for r in range(4):
+            load_scale_rows(nc.sync, w3s, w3_scales, r)
 
-        logs(((1, 0), (0, 0), (1, 1), (0, 1)))
+        for t in (0, 1):
+            logs(t)
         for t in (0, 1):
             softplus(t)
             queue(t)
-        share_b(0)
-        share_q(0)
+        share(den[0], btl[0])
+        share(qs[0], q[0])
         for t, slot in ((3, 0), (2, 1)):
-            open_banks(t, slot)
             for a in range(2):
-                for k in range(len(WORD_PIECES)):
-                    product(t, a, k)
                 for h in range(2):
-                    sigmoid(t, a, h * BANK, (h + 1) * BANK)
-        logs(((1, 2), (0, 2), (1, 3), (0, 3)))
+                    product(t, a, h, slot)
+                    sigmoid(t, a, h)
+        for t in (2, 3):
+            logs(t)
         denominator(0)
-        pairs(0)
-        share_b(1)
-        share_q(1)
-        denominator(1)
+        cross(0)
+        weigh(0, nc.vector)
+        pair_sum(0)
+        numerator(0)
+        share(qs[1], q[1])
+        denominator_fused(1)
         for t in (2, 3):
             softplus(t)
             queue(t)
         for t in (2, 3):
-            share_b(t)
-            share_q(t)
-
-        pairs(1)
-        for t in (2, 3):
-            denominator(t)
-            pairs(t)
+            share(den[t], btl[t])
+            share(qs[t], q[t])
+        for t in (1, 2, 3):
+            if t != FUSED_TILE:
+                denominator(t)
+            cross(t)
+            weigh(t, nc.vector)
+            pair_sum(t)
         for t in range(PACK):
             log_pair(t)
-        for t in range(PACK):
+        for t in (1, 2, 3):
             numerator(t)
-        for k in range(len(OUT_PIECES)):
-            finish(k)
+        hidden(0)
+        for k in range(1, len(OUT_PIECES)):
+            hidden(k)
+            finish(k - 1)
+        finish(len(OUT_PIECES) - 1)

@@ -36,27 +36,24 @@ def tile_picked_ytcpcc_shr_p_kernel(tc, x_words, x_scales, w1_words, w1_scales, 
 
         offs_sb = keep.tile([P, S // 16], U16, name="offs_sb")
         shr_sb = keep.tile([P, S // 16], U16, name="shr_sb")
-        xw = keep.tile([P, T], U32, name="xw", tag="xw", align_bytes=64)
+        xw = keep.tile([P, T], U32, name="xw", align_bytes=64)
         xs = keep.tile([P, T], U8, name="xs", align_bytes=64)
         ww = [keep.tile([P, 2 * H], U8, name=f"ww{a}", tag=f"raw{a}", align_bytes=64) for a in range(2)]
         ws = [keep.tile([P, H], U8, name=f"ws{a}", tag=f"raw{2 + a}", align_bytes=64) for a in range(2)]
 
+        nc.vector.memset(ws[0][:].bitcast(I32), 0)
+        nc.vector.memset(ws[1][:].bitcast(I32), 0)
         nc.vector.memset(xs[:].bitcast(I32), 0)
-        nc.gpsimd.memset(ws[0][:].bitcast(I32), 0)
-        nc.gpsimd.memset(ws[1][:].bitcast(I32), 0)
 
-        both = (nc.sync, nc.scalar)
         nc.sync.dma_start(out=offs_sb[:], in_=offs)
-        nc.scalar.dma_start(out=ww[0][:].bitcast(I32), in_=w1_words[0].bitcast(I32))
-        for r in range(4):
-            load_scale_rows(both[r % 2], xs, x_scales, r)
-        load_scale_rows(nc.sync, ws[0], w1_scales, 0)
         nc.scalar.dma_start(out=xw[:].bitcast(I32), in_=x_words[0].rearrange("p n t -> p (n t)").bitcast(I32))
-        for r in range(1, 4):
-            load_scale_rows(both[(r + 1) % 2], ws[0], w1_scales, r)
-        nc.scalar.dma_start(out=ww[1][:].bitcast(I32), in_=w2_words[0].bitcast(I32))
+        nc.sync.dma_start(out=ww[0][:].bitcast(I32), in_=w1_words[0].bitcast(I32))
+        nc.sync.dma_start(out=ww[1][:].bitcast(I32), in_=w2_words[0].bitcast(I32))
         for r in range(4):
-            load_scale_rows(nc.scalar if r == 1 else nc.sync, ws[1], w2_scales, r)
+            load_scale_rows(nc.scalar, ws[0], w1_scales, r)
+            load_scale_rows(nc.sync, ws[1], w2_scales, r)
+        for r in range(4):
+            load_scale_rows((nc.scalar, nc.sync)[r % 2], xs, x_scales, r)
         nc.sync.dma_start(out=shr_sb[:], in_=shr)
 
         dw = {}
@@ -104,15 +101,19 @@ def tile_picked_ytcpcc_shr_p_kernel(tc, x_words, x_scales, w1_words, w1_scales, 
         def sigmoid(t, a, h):
             nc.scalar.activation(out=sg[t][:, a, halves[h]], in_=banks[t, a, h][:], func=ACT.Sigmoid, scale=-1.0)
 
+        def log_pieces(t):
+            return ((0, 256), (256, 512), (512, 1024)) if t % 2 == 0 else ((0, 512), (512, 1024))
+
         def logs(t):
-            for h in range(2):
-                nc.scalar.activation(out=sg[t][:, :, halves[h]], in_=sg[t][:, :, halves[h]], func=ACT.Ln, bias=TINY)
+            for lo, hi in log_pieces(t):
+                nc.scalar.activation(out=sg[t][:, :, lo:hi], in_=sg[t][:, :, lo:hi], func=ACT.Ln, bias=TINY)
 
         def softplus(t):
-            for h in range(2):
-                for a, dst in ((1, sg[t][:, 1, halves[h]]), (0, btl[t][:, halves[h]])):
-                    nc.vector.scalar_tensor_tensor(out=dst, in0=sg[t][:, a, halves[h]], scalar=-1.0,
-                                                   in1=banks[t, a, h][:], op0=ALU.mult, op1=ALU.max)
+            for lo, hi in log_pieces(t):
+                h = lo // HALF
+                for a, dst in ((1, sg[t][:, 1, lo:hi]), (0, btl[t][:, lo:hi])):
+                    nc.vector.scalar_tensor_tensor(out=dst, in0=sg[t][:, a, lo:hi], scalar=-1.0,
+                                                   in1=banks[t, a, h][:, lo - h * HALF : hi - h * HALF], op0=ALU.mult, op1=ALU.max)
 
         def queue(t):
             for c in halves:
@@ -196,39 +197,27 @@ def tile_picked_ytcpcc_shr_p_kernel(tc, x_words, x_scales, w1_words, w1_scales, 
             for t in (1, 0):
                 sigmoid(t, a, h)
 
-        deal_words(nc.vector, 0, 0)
-        pick_scales(0)
-        deal_scales(nc.vector, 0, 0)
-        pick_words(0)
-        first_products(0, 0)
-        pick_scales(1)
-        pick_words(1)
-        first_products(0, 1)
-        deal_words(nc.vector, 1, 0)
-        deal_scales(nc.vector, 1, 0)
-        first_products(1, 0)
-        first_products(1, 1)
-
-        late = keep.tile([P, 12 * P], U8, name="late", tag="xw", align_bytes=64)
         for a in range(2):
-            dw[a, 1] = late[:, 6 * P * a : 6 * P * a + 4 * P]
-            ds[a, 1] = late[:, 6 * P * a + 4 * P : 6 * P * (a + 1)]
-            deal_words(nc.gpsimd, a, 1)
-            deal_scales(nc.gpsimd, a, 1)
+            deal_words(nc.vector, a, 0)
+        for a in range(2):
+            deal_scales(nc.vector, a, 0)
+        for h in range(2):
+            pick_words(h)
+        for h in range(2):
+            pick_scales(h)
+            for a in range(2):
+                first_products(a, h)
+
+        for a in range(2):
+            dw[a, 1] = keep.tile([P, 4 * P], U8, name=f"dw{a}_late", tag=f"dw{a}", align_bytes=64)[:]
+            ds[a, 1] = keep.tile([P, 2 * P], U8, name=f"ds{a}_late", tag=f"ds{a}", align_bytes=64)[:]
+            deal_words(nc.vector, a, 1)
+            deal_scales(nc.vector, a, 1)
 
         infl_rows = infl.rearrange("(p t) j -> p t j", t=PACK)
         q = [keep.tile([P, S], F32, name=f"q{t}", tag=f"raw{(0, 2, 1, 3)[t]}", align_bytes=64) for t in range(PACK)]
         for t in range(PACK):
             nc.sync.dma_start(out=q[t][:], in_=infl_rows[:, t, :])
-        unit_sb = keep.tile([P, PACK], F32, name="unit_sb", tag="ds0", align_bytes=64)
-        w3w = keep.tile([P, 2 * N], U8, name="w3w", tag="dw0", align_bytes=64)
-        w3s = keep.tile([P, N], U8, name="w3s", tag="dw1", align_bytes=64)
-        nc.sync.dma_start(out=unit_sb[:], in_=unit.rearrange("(p t) o -> p (t o)", t=PACK))
-        nc.sync.dma_start(out=w3w[:].bitcast(I32), in_=w3_words[0].bitcast(I32))
-        nc.gpsimd.memset(w3s[:].bitcast(I32), 0)
-        for r in range(4):
-            load_scale_rows(nc.sync, w3s, w3_scales, r)
-
         for t in (0, 1):
             logs(t)
         for t in (0, 1):
@@ -241,6 +230,15 @@ def tile_picked_ytcpcc_shr_p_kernel(tc, x_words, x_scales, w1_words, w1_scales, 
                 for h in range(2):
                     product(t, a, h, slot)
                     sigmoid(t, a, h)
+        unit_sb = keep.tile([P, PACK], F32, name="unit_sb", tag="ds0", align_bytes=64)
+        w3w = keep.tile([P, 2 * N], U8, name="w3w", tag="dw0", align_bytes=64)
+        w3s = keep.tile([P, N], U8, name="w3s", tag="dw1", align_bytes=64)
+        nc.sync.dma_start(out=unit_sb[:], in_=unit.rearrange("(p t) o -> p (t o)", t=PACK))
+        nc.sync.dma_start(out=w3w[:].bitcast(I32), in_=w3_words[0].bitcast(I32))
+        nc.vector.memset(w3s[:].bitcast(I32), 0)
+        for r in range(4):
+            load_scale_rows(nc.sync, w3s, w3_scales, r)
+
         for t in (2, 3):
             logs(t)
         denominator(0)

@@ -15,15 +15,21 @@ ALU = mybir.AluOpType
 
 K, T, S, H, N = 512, 2048, 1024, 512, 128
 FLOPS = 2 * K * H * S * 2 + 2 * H * N * S
+
 P = 128
 PACK = 4
 HALF = 512
 TINY = 2.0 ** -60
+BW, RT = 0, 1
+LOG_PIECES_FIRST = ((0, 256), (256, 512), (512, 1024))
+LOG_PIECES_SECOND = ((0, 512), (512, 1024))
 OUT_PIECES = ((0, 256), (256, 512), (512, 768), (768, 896), (896, 1024))
-FUSED_TILE = 1
+VECTOR_GATHER_TILE = 1
 
 
-def tile_picked_ytcpcc_shr_p_kernel(tc, x_words, x_scales, w1_words, w1_scales, w2_words, w2_scales, infl, unit, w3_words, w3_scales, offs, shr, out):
+def tile_picked_ytcpcc_shr_p_kernel(
+    tc, x_words, x_scales, w1_words, w1_scales, w2_words, w2_scales, infl, unit, w3_words, w3_scales, offs, shr, out
+):
     nc = tc.nc
     halves = [slice(h * HALF, (h + 1) * HALF) for h in range(2)]
     list_halves = [slice(h * HALF // 16, (h + 1) * HALF // 16) for h in range(2)]
@@ -36,147 +42,175 @@ def tile_picked_ytcpcc_shr_p_kernel(tc, x_words, x_scales, w1_words, w1_scales, 
 
         offs_sb = keep.tile([P, S // 16], U16, name="offs_sb")
         shr_sb = keep.tile([P, S // 16], U16, name="shr_sb")
-        xw = keep.tile([P, T], U32, name="xw", align_bytes=64)
-        xs = keep.tile([P, T], U8, name="xs", align_bytes=64)
-        ww = [keep.tile([P, 2 * H], U8, name=f"ww{a}", tag=f"raw{a}", align_bytes=64) for a in range(2)]
-        ws = [keep.tile([P, H], U8, name=f"ws{a}", tag=f"raw{2 + a}", align_bytes=64) for a in range(2)]
+        x_word_table = keep.tile([P, T], U32, name="x_word_table", align_bytes=64)
+        x_scale_table = keep.tile([P, T], U8, name="x_scale_table", align_bytes=64)
+        w_words = [keep.tile([P, 2 * H], U8, name=f"w_words{a}", tag=f"raw{a}", align_bytes=64) for a in (BW, RT)]
+        w_scales = [keep.tile([P, H], U8, name=f"w_scales{a}", tag=f"raw{2 + a}", align_bytes=64) for a in (BW, RT)]
 
-        nc.vector.memset(ws[0][:].bitcast(I32), 0)
-        nc.vector.memset(ws[1][:].bitcast(I32), 0)
-        nc.vector.memset(xs[:].bitcast(I32), 0)
+        nc.vector.memset(x_scale_table[:].bitcast(I32), 0)
+        nc.vector.memset(w_scales[BW][:].bitcast(I32), 0)
+        nc.vector.memset(w_scales[RT][:].bitcast(I32), 0)
 
         nc.sync.dma_start(out=offs_sb[:], in_=offs)
-        nc.scalar.dma_start(out=xw[:].bitcast(I32), in_=x_words[0].rearrange("p n t -> p (n t)").bitcast(I32))
-        nc.sync.dma_start(out=ww[0][:].bitcast(I32), in_=w1_words[0].bitcast(I32))
-        nc.sync.dma_start(out=ww[1][:].bitcast(I32), in_=w2_words[0].bitcast(I32))
+        nc.scalar.dma_start(out=w_words[BW][:].bitcast(I32), in_=w1_words[0].bitcast(I32))
+        nc.scalar.dma_start(out=w_words[RT][:].bitcast(I32), in_=w2_words[0].bitcast(I32))
         for r in range(4):
-            load_scale_rows(nc.scalar, ws[0], w1_scales, r)
-            load_scale_rows(nc.sync, ws[1], w2_scales, r)
-        for r in range(4):
-            load_scale_rows((nc.scalar, nc.sync)[r % 2], xs, x_scales, r)
+            load_scale_rows((nc.sync, nc.scalar)[r % 2], x_scale_table, x_scales, r)
+        nc.scalar.dma_start(out=x_word_table[:].bitcast(I32), in_=x_words[0].rearrange("p n t -> p (n t)").bitcast(I32))
+        for a, rows in ((BW, w1_scales), (RT, w2_scales)):
+            for r in range(4):
+                load_scale_rows(nc.sync, w_scales[a], rows, r)
         nc.sync.dma_start(out=shr_sb[:], in_=shr)
 
-        dw = {}
-        ds = {}
+        dealt_words = {}
+        dealt_scales = {}
 
-        def deal_words(engine, a, g):
-            engine.tensor_copy(out=dw[a, g].rearrange("p (t m b) -> p t m b", t=2, b=2),
-                               in_=ww[a][:].rearrange("p (m t b) -> p t m b", t=PACK, b=2)[:, 2 * g : 2 * g + 2])
+        def open_dealt(a, g):
+            dealt_words[a, g] = keep.tile([P, 4 * P], U8, name=f"dealt_words{a}_{g}", tag=f"dealt_words{a}", align_bytes=64)
+            dealt_scales[a, g] = keep.tile([P, 2 * P], U8, name=f"dealt_scales{a}_{g}", tag=f"dealt_scales{a}", align_bytes=64)
 
-        def deal_scales(engine, a, g):
-            engine.tensor_copy(out=ds[a, g].rearrange("p (t m) -> p t m", t=2),
-                               in_=ws[a][:].rearrange("p (m t) -> p t m", t=PACK)[:, 2 * g : 2 * g + 2])
+        def deal_words(a, g):
+            nc.vector.tensor_copy(
+                out=dealt_words[a, g][:].rearrange("p (t m b) -> p t m b", t=2, b=2),
+                in_=w_words[a][:].rearrange("p (m t b) -> p t m b", t=PACK, b=2)[:, 2 * g : 2 * g + 2],
+            )
 
-        for a in range(2):
-            dw[a, 0] = keep.tile([P, 4 * P], U8, name=f"dw{a}", tag=f"dw{a}", align_bytes=64)[:]
-            ds[a, 0] = keep.tile([P, 2 * P], U8, name=f"ds{a}", tag=f"ds{a}", align_bytes=64)[:]
+        def deal_scales(a, g):
+            nc.vector.tensor_copy(
+                out=dealt_scales[a, g][:].rearrange("p (t m) -> p t m", t=2),
+                in_=w_scales[a][:].rearrange("p (m t) -> p t m", t=PACK)[:, 2 * g : 2 * g + 2],
+            )
 
-        gw = [keep.tile([P, HALF], U32, name=f"gw{h}", align_bytes=64) for h in range(2)]
-        gs = [keep.tile([P, HALF], U8, name=f"gs{h}", align_bytes=64) for h in range(2)]
+        for a in (BW, RT):
+            open_dealt(a, 0)
+
+        picked_words = [keep.tile([P, HALF], U32, name=f"picked_words{h}", align_bytes=64) for h in range(2)]
+        picked_scales = [keep.tile([P, HALF], U8, name=f"picked_scales{h}", align_bytes=64) for h in range(2)]
 
         def pick_scales(h):
-            nc.vector.tensor_copy(out=gs[h][:], in_=xs[:].indirect(offs_sb[:, list_halves[h]]))
+            nc.vector.tensor_copy(out=picked_scales[h][:], in_=x_scale_table[:].indirect(offs_sb[:, list_halves[h]]))
 
         def pick_words(h):
-            nc.vector.tensor_copy(out=gw[h][:], in_=xw[:].indirect(offs_sb[:, list_halves[h]]))
+            nc.vector.tensor_copy(out=picked_words[h][:], in_=x_word_table[:].indirect(offs_sb[:, list_halves[h]]))
 
-        sg = [keep.tile([P, 2, S], F32, name=f"sg{t}") for t in range(PACK)]
+        soft = [keep.tile([P, 2, S], F32, name=f"soft{t}") for t in range(PACK)]
         btl = [keep.tile([P, S], F32, name=f"btl{t}") for t in range(PACK)]
         bdp = [keep.tile([P, S], F32, name=f"bdp{t}") for t in range(PACK)]
-        qs = [keep.tile([P, S], F32, name=f"qs{t}") for t in range(PACK)]
+        cross = [keep.tile([P, S], F32, name=f"cross{t}") for t in range(PACK)]
         den = [keep.tile([P, S], F32, name=f"den{t}") for t in range(PACK)]
-        que5 = keep.tile([P, S], F32, name="que5")
-        pair = [keep.tile([P, S // 2], F32, name=f"pair{t}") for t in range(PACK)]
-        lnp = keep.tile([P, PACK, S // 2], F32, name="lnp")
+        que_half = keep.tile([P, S], F32, name="que_half")
+        pairsum = [keep.tile([P, S // 2], F32, name=f"pairsum{t}") for t in range(PACK)]
+        log_pairsum = keep.tile([P, PACK, S // 2], F32, name="log_pairsum")
         top = keep.tile([P, PACK, S], F32, name="top")
         banks = {}
 
         def product(t, a, h, slot):
             banks[t, a, h] = psum.tile([P, HALF], F32, name=f"acc{t}_{a}_{h}", tag=f"bank{slot}_{a}_{h}")
             g, i = divmod(t, 2)
-            nc.tensor.matmul_mx(out=banks[t, a, h][:], lhsT=dw[a, g][:, 2 * P * i : 2 * P * (i + 1)].bitcast(FP4X4),
-                                lhsT_scale=ds[a, g][:, P * i : P * (i + 1)],
-                                rhs=gw[h][:].bitcast(FP8X4), rhs_scale=gs[h][:], start=True, stop=True)
+            nc.tensor.matmul_mx(
+                out=banks[t, a, h][:],
+                lhsT=dealt_words[a, g][:, 2 * P * i : 2 * P * (i + 1)].bitcast(FP4X4),
+                lhsT_scale=dealt_scales[a, g][:, P * i : P * (i + 1)],
+                rhs=picked_words[h][:].bitcast(FP8X4),
+                rhs_scale=picked_scales[h][:],
+                start=True,
+                stop=True,
+            )
 
         def sigmoid(t, a, h):
-            nc.scalar.activation(out=sg[t][:, a, halves[h]], in_=banks[t, a, h][:], func=ACT.Sigmoid, scale=-1.0)
+            nc.scalar.activation(out=soft[t][:, a, halves[h]], in_=banks[t, a, h][:], func=ACT.Sigmoid, scale=-1.0)
 
         def log_pieces(t):
-            return ((0, 256), (256, 512), (512, 1024)) if t % 2 == 0 else ((0, 512), (512, 1024))
+            return LOG_PIECES_FIRST if t % 2 == 0 else LOG_PIECES_SECOND
 
         def logs(t):
             for lo, hi in log_pieces(t):
-                nc.scalar.activation(out=sg[t][:, :, lo:hi], in_=sg[t][:, :, lo:hi], func=ACT.Ln, bias=TINY)
+                nc.scalar.activation(out=soft[t][:, :, lo:hi], in_=soft[t][:, :, lo:hi], func=ACT.Ln, bias=TINY)
 
         def softplus(t):
             for lo, hi in log_pieces(t):
                 h = lo // HALF
-                for a, dst in ((1, sg[t][:, 1, lo:hi]), (0, btl[t][:, lo:hi])):
-                    nc.vector.scalar_tensor_tensor(out=dst, in0=sg[t][:, a, lo:hi], scalar=-1.0,
-                                                   in1=banks[t, a, h][:, lo - h * HALF : hi - h * HALF], op0=ALU.mult, op1=ALU.max)
+                for a, dst in ((RT, soft[t][:, RT, lo:hi]), (BW, btl[t][:, lo:hi])):
+                    nc.vector.scalar_tensor_tensor(
+                        out=dst, in0=soft[t][:, a, lo:hi], scalar=-1.0,
+                        in1=banks[t, a, h][:, lo - h * HALF : hi - h * HALF], op0=ALU.mult, op1=ALU.max,
+                    )
 
-        def queue(t):
+        def overflow(t):
             for c in halves:
-                nc.vector.scalar_tensor_tensor(out=bdp[t][:, c], in0=sg[t][:, 1, c], scalar=0.3, in1=btl[t][:, c],
-                                               op0=ALU.add, op1=ALU.mult)
+                nc.vector.scalar_tensor_tensor(
+                    out=bdp[t][:, c], in0=soft[t][:, RT, c], scalar=0.3, in1=btl[t][:, c], op0=ALU.add, op1=ALU.mult
+                )
             for c in halves:
-                nc.vector.scalar_tensor_tensor(out=q[t][:, c], in0=bdp[t][:, c], scalar=-0.7, in1=q[t][:, c],
-                                               op0=ALU.mult, op1=ALU.add)
+                nc.vector.scalar_tensor_tensor(
+                    out=over[t][:, c], in0=bdp[t][:, c], scalar=-0.7, in1=over[t][:, c], op0=ALU.mult, op1=ALU.add
+                )
 
-        def share(dst, src):
+        def share(dst, window):
             for h in range(2):
-                nc.scalar.activation(out=dst[:, halves[h]], in_=src[:].indirect(shr_sb[:, list_halves[h]]),
-                                     func=ACT.Copy, bias=0.5)
+                nc.scalar.activation(
+                    out=dst[:, halves[h]], in_=window[:].indirect(shr_sb[:, list_halves[h]]), func=ACT.Copy, bias=0.5
+                )
 
         def denominator(t):
             for c in halves:
-                nc.vector.scalar_tensor_tensor(out=den[t][:, c], in0=q[t][:, c], scalar=0.0, in1=den[t][:, c],
-                                               op0=ALU.max, op1=ALU.add)
+                nc.vector.scalar_tensor_tensor(
+                    out=den[t][:, c], in0=over[t][:, c], scalar=0.0, in1=den[t][:, c], op0=ALU.max, op1=ALU.add
+                )
 
-        def denominator_fused(t):
+        def denominator_with_gather(t):
             for c in halves:
-                nc.vector.tensor_scalar(out=que5[:, c], in0=q[t][:, c], scalar1=0.0, scalar2=0.5, op0=ALU.max, op1=ALU.add)
+                nc.vector.tensor_scalar(
+                    out=que_half[:, c], in0=over[t][:, c], scalar1=0.0, scalar2=0.5, op0=ALU.max, op1=ALU.add
+                )
             for h in range(2):
-                nc.vector.tensor_tensor(out=den[t][:, halves[h]], in0=btl[t][:].indirect(shr_sb[:, list_halves[h]]),
-                                        in1=que5[:, halves[h]], op=ALU.add)
+                nc.vector.tensor_tensor(
+                    out=den[t][:, halves[h]], in0=btl[t][:].indirect(shr_sb[:, list_halves[h]]),
+                    in1=que_half[:, halves[h]], op=ALU.add,
+                )
 
         def by_pairs(ap):
             return ap.rearrange("p (v d) -> p v d", d=2)
 
-        def cross(t):
+        def pair_sums(t):
             for c in halves:
-                nc.vector.scalar_tensor_tensor(out=by_pairs(qs[t][:, c]), in0=by_pairs(qs[t][:, c]), scalar=0.5,
-                                               in1=by_pairs(den[t][:, c])[:, :, ::-1], op0=ALU.max, op1=ALU.mult)
-
-        def weigh(t, engine):
+                nc.vector.scalar_tensor_tensor(
+                    out=by_pairs(cross[t][:, c]), in0=by_pairs(cross[t][:, c]), scalar=0.5,
+                    in1=by_pairs(den[t][:, c])[:, :, ::-1], op0=ALU.max, op1=ALU.mult,
+                )
             for c in halves:
-                engine.tensor_tensor(out=den[t][:, c], in0=btl[t][:, c], in1=qs[t][:, c], op=ALU.mult)
-
-        def pair_sum(t):
+                nc.vector.tensor_tensor(out=den[t][:, c], in0=btl[t][:, c], in1=cross[t][:, c], op=ALU.mult)
             for h in range(2):
-                m = by_pairs(den[t][:, halves[h]])
-                nc.vector.tensor_tensor(out=pair[t][:, h * HALF // 2 : (h + 1) * HALF // 2], in0=m[:, :, 0], in1=m[:, :, 1], op=ALU.add)
-
-        def log_pair(t):
-            nc.scalar.activation(out=lnp[:, t, :], in_=pair[t][:], func=ACT.Ln)
+                members = by_pairs(den[t][:, halves[h]])
+                nc.vector.tensor_tensor(
+                    out=pairsum[t][:, h * HALF // 2 : (h + 1) * HALF // 2],
+                    in0=members[:, :, 0], in1=members[:, :, 1], op=ALU.add,
+                )
 
         def numerator(t):
             for c in halves:
-                nc.vector.scalar_tensor_tensor(out=top[:, t, c], in0=bdp[t][:, c], scalar=unit_sb[:, t : t + 1], in1=qs[t][:, c],
-                                               op0=ALU.mult, op1=ALU.mult)
+                nc.vector.scalar_tensor_tensor(
+                    out=top[:, t, c], in0=bdp[t][:, c], scalar=unit_sb[:, t : t + 1], in1=cross[t][:, c],
+                    op0=ALU.mult, op1=ALU.mult,
+                )
 
         hid = {}
 
         def hidden(k):
             lo, hi = OUT_PIECES[k]
             n = hi - lo
-            rec = keep.tile([P, n // 2, PACK], F32, name=f"rec{k}")
-            nc.scalar.activation(out=rec[:], in_=lnp[:, :, lo // 2 : hi // 2].rearrange("p t v -> p v t"),
-                                 func=ACT.Exp, scale=-1.0)
+            inverse = keep.tile([P, n // 2, PACK], F32, name=f"inverse{k}")
+            nc.scalar.activation(
+                out=inverse[:], in_=log_pairsum[:, :, lo // 2 : hi // 2].rearrange("p t v -> p v t"),
+                func=ACT.Exp, scale=-1.0,
+            )
             hid[k] = keep.tile([P, n * PACK], BF16, name=f"hid{k}", align_bytes=64)
-            nc.vector.tensor_tensor(out=hid[k][:].rearrange("p (v d t) -> p v t d", d=2, t=PACK),
-                                    in0=top[:, :, lo:hi].rearrange("p t (v d) -> p v t d", d=2),
-                                    in1=rec[:].unsqueeze(3).to_broadcast([P, n // 2, PACK, 2]), op=ALU.mult)
+            nc.vector.tensor_tensor(
+                out=hid[k][:].rearrange("p (v d t) -> p v t d", d=2, t=PACK),
+                in0=top[:, :, lo:hi].rearrange("p t (v d) -> p v t d", d=2),
+                in1=inverse[:].unsqueeze(3).to_broadcast([P, n // 2, PACK, 2]),
+                op=ALU.mult,
+            )
 
         def finish(k):
             lo, hi = OUT_PIECES[k]
@@ -185,85 +219,87 @@ def tile_picked_ytcpcc_shr_p_kernel(tc, x_words, x_scales, w1_words, w1_scales, 
             scales = keep.tile([P, n], U8, name=f"scales{k}", align_bytes=64)
             nc.vector.quantize_mx(out=codes[:].bitcast(FP8X4), scales=scales[:], in_=hid[k][:])
             acc = psum.tile([P, n], F32, name=f"res{k}", tag=f"bank{k // 4}_{k // 2 % 2}_{k % 2}")
-            nc.tensor.matmul_mx(out=acc[:], lhsT=w3w[:].bitcast(FP4X4), lhsT_scale=w3s[:],
-                                rhs=codes[:].bitcast(FP8X4), rhs_scale=scales[:], start=True, stop=True)
+            nc.tensor.matmul_mx(
+                out=acc[:], lhsT=w3_word_sb[:].bitcast(FP4X4), lhsT_scale=w3_scale_sb[:],
+                rhs=codes[:].bitcast(FP8X4), rhs_scale=scales[:], start=True, stop=True,
+            )
             res = keep.tile([P, n], F32, name=f"out{k}")
             nc.scalar.copy(out=res[:], in_=acc[:])
             nc.sync.dma_start(out=out[:, lo:hi], in_=res[:])
 
-        def first_products(a, h):
-            for t in (1, 0):
-                product(t, a, h, t)
-            for t in (1, 0):
-                sigmoid(t, a, h)
-
-        for a in range(2):
-            deal_words(nc.vector, a, 0)
-        for a in range(2):
-            deal_scales(nc.vector, a, 0)
-        for h in range(2):
-            pick_words(h)
+        for a in (BW, RT):
+            deal_words(a, 0)
         for h in range(2):
             pick_scales(h)
-            for a in range(2):
-                first_products(a, h)
+        deal_scales(BW, 0)
+        pick_words(0)
+        deal_scales(RT, 0)
+        pick_words(1)
+        for a in (BW, RT):
+            for h in range(2):
+                for t in (1, 0):
+                    product(t, a, h, t)
+                for t in (1, 0):
+                    sigmoid(t, a, h)
 
-        for a in range(2):
-            dw[a, 1] = keep.tile([P, 4 * P], U8, name=f"dw{a}_late", tag=f"dw{a}", align_bytes=64)[:]
-            ds[a, 1] = keep.tile([P, 2 * P], U8, name=f"ds{a}_late", tag=f"ds{a}", align_bytes=64)[:]
-            deal_words(nc.vector, a, 1)
-            deal_scales(nc.vector, a, 1)
+        for a in (BW, RT):
+            open_dealt(a, 1)
+            deal_words(a, 1)
+            deal_scales(a, 1)
 
         infl_rows = infl.rearrange("(p t) j -> p t j", t=PACK)
-        q = [keep.tile([P, S], F32, name=f"q{t}", tag=f"raw{(0, 2, 1, 3)[t]}", align_bytes=64) for t in range(PACK)]
+        over = [
+            keep.tile([P, S], F32, name=f"over{t}", tag=tag, align_bytes=64)
+            for t, tag in enumerate(("raw0", "raw2", "raw1", "raw3"))
+        ]
         for t in range(PACK):
-            nc.sync.dma_start(out=q[t][:], in_=infl_rows[:, t, :])
+            nc.sync.dma_start(out=over[t][:], in_=infl_rows[:, t, :])
+
         for t in (0, 1):
             logs(t)
         for t in (0, 1):
             softplus(t)
-            queue(t)
+            overflow(t)
         share(den[0], btl[0])
-        share(qs[0], q[0])
+        share(cross[0], over[0])
+
         for t, slot in ((3, 0), (2, 1)):
-            for a in range(2):
+            for a in (BW, RT):
                 for h in range(2):
                     product(t, a, h, slot)
                     sigmoid(t, a, h)
-        unit_sb = keep.tile([P, PACK], F32, name="unit_sb", tag="ds0", align_bytes=64)
-        w3w = keep.tile([P, 2 * N], U8, name="w3w", tag="dw0", align_bytes=64)
-        w3s = keep.tile([P, N], U8, name="w3s", tag="dw1", align_bytes=64)
+
+        unit_sb = keep.tile([P, PACK], F32, name="unit_sb", tag="dealt_scales0", align_bytes=64)
+        w3_word_sb = keep.tile([P, 2 * N], U8, name="w3_word_sb", tag="dealt_words0", align_bytes=64)
+        w3_scale_sb = keep.tile([P, N], U8, name="w3_scale_sb", tag="dealt_words1", align_bytes=64)
         nc.sync.dma_start(out=unit_sb[:], in_=unit.rearrange("(p t) o -> p (t o)", t=PACK))
-        nc.sync.dma_start(out=w3w[:].bitcast(I32), in_=w3_words[0].bitcast(I32))
-        nc.vector.memset(w3s[:].bitcast(I32), 0)
+        nc.sync.dma_start(out=w3_word_sb[:].bitcast(I32), in_=w3_words[0].bitcast(I32))
+        nc.vector.memset(w3_scale_sb[:].bitcast(I32), 0)
         for r in range(4):
-            load_scale_rows(nc.sync, w3s, w3_scales, r)
+            load_scale_rows(nc.sync, w3_scale_sb, w3_scales, r)
 
         for t in (2, 3):
             logs(t)
         denominator(0)
-        cross(0)
-        weigh(0, nc.vector)
-        pair_sum(0)
+        pair_sums(0)
         numerator(0)
-        share(qs[1], q[1])
-        denominator_fused(1)
+        share(cross[VECTOR_GATHER_TILE], over[VECTOR_GATHER_TILE])
+        denominator_with_gather(VECTOR_GATHER_TILE)
         for t in (2, 3):
             softplus(t)
-            queue(t)
+            overflow(t)
         for t in (2, 3):
             share(den[t], btl[t])
-            share(qs[t], q[t])
+            share(cross[t], over[t])
         for t in (1, 2, 3):
-            if t != FUSED_TILE:
+            if t != VECTOR_GATHER_TILE:
                 denominator(t)
-            cross(t)
-            weigh(t, nc.vector)
-            pair_sum(t)
+            pair_sums(t)
         for t in range(PACK):
-            log_pair(t)
+            nc.scalar.activation(out=log_pairsum[:, t, :], in_=pairsum[t][:], func=ACT.Ln)
         for t in (1, 2, 3):
             numerator(t)
+
         hidden(0)
         for k in range(1, len(OUT_PIECES)):
             hidden(k)

from contextlib import ExitStack

import concourse.mybir as mybir

F32 = mybir.dt.float32
BF16 = mybir.dt.bfloat16
I32 = mybir.dt.int32
U32 = mybir.dt.uint32
U16 = mybir.dt.uint16
U8 = mybir.dt.uint8
FP8X4 = mybir.dt.float8_e4m3fn_x4
FP4X4 = mybir.dt.float4_e2m1fn_x4
ACT = mybir.ActivationFunctionType
ALU = mybir.AluOpType

K, T, S, H, N = 512, 2048, 1024, 512, 128
FLOPS = 2 * K * H * S * 2 + 2 * H * N * S

P = 128
PACK = 4
HALF = 512
TINY = 2.0 ** -60
BW, RT = 0, 1
LOG_PIECES_FIRST = ((0, 256), (256, 512), (512, 1024))
LOG_PIECES_SECOND = ((0, 512), (512, 1024))
OUT_PIECES = ((0, 256), (256, 512), (512, 768), (768, 896), (896, 1024))
VECTOR_GATHER_TILE = 1


def tile_picked_ytcpcc_shr_p_kernel(
    tc, x_words, x_scales, w1_words, w1_scales, w2_words, w2_scales, infl, unit, w3_words, w3_scales, offs, shr, out
):
    nc = tc.nc
    halves = [slice(h * HALF, (h + 1) * HALF) for h in range(2)]
    list_halves = [slice(h * HALF // 16, (h + 1) * HALF // 16) for h in range(2)]
    with ExitStack() as ctx:
        keep = ctx.enter_context(tc.tile_pool(name="keep", bufs=1))
        psum = ctx.enter_context(tc.psum_pool(name="psum", bufs=1))

        def load_scale_rows(queue, plane, rows, r):
            queue.dma_start(out=plane[r:P:32, :].bitcast(I32), in_=rows[0][r:16:4, :].bitcast(I32))

        offs_sb = keep.tile([P, S // 16], U16, name="offs_sb")
        shr_sb = keep.tile([P, S // 16], U16, name="shr_sb")
        x_word_table = keep.tile([P, T], U32, name="x_word_table", align_bytes=64)
        x_scale_table = keep.tile([P, T], U8, name="x_scale_table", align_bytes=64)
        w_words = [keep.tile([P, 2 * H], U8, name=f"w_words{a}", tag=f"raw{a}", align_bytes=64) for a in (BW, RT)]
        w_scales = [keep.tile([P, H], U8, name=f"w_scales{a}", tag=f"raw{2 + a}", align_bytes=64) for a in (BW, RT)]

        nc.vector.memset(x_scale_table[:].bitcast(I32), 0)
        nc.vector.memset(w_scales[BW][:].bitcast(I32), 0)
        nc.vector.memset(w_scales[RT][:].bitcast(I32), 0)

        nc.sync.dma_start(out=offs_sb[:], in_=offs)
        nc.scalar.dma_start(out=w_words[BW][:].bitcast(I32), in_=w1_words[0].bitcast(I32))
        nc.scalar.dma_start(out=w_words[RT][:].bitcast(I32), in_=w2_words[0].bitcast(I32))
        for r in range(4):
            load_scale_rows((nc.sync, nc.scalar)[r % 2], x_scale_table, x_scales, r)
        nc.scalar.dma_start(out=x_word_table[:].bitcast(I32), in_=x_words[0].rearrange("p n t -> p (n t)").bitcast(I32))
        for a, rows in ((BW, w1_scales), (RT, w2_scales)):
            for r in range(4):
                load_scale_rows(nc.sync, w_scales[a], rows, r)
        nc.sync.dma_start(out=shr_sb[:], in_=shr)

        dealt_words = {}
        dealt_scales = {}

        def open_dealt(a, g):
            dealt_words[a, g] = keep.tile([P, 4 * P], U8, name=f"dealt_words{a}_{g}", tag=f"dealt_words{a}", align_bytes=64)
            dealt_scales[a, g] = keep.tile([P, 2 * P], U8, name=f"dealt_scales{a}_{g}", tag=f"dealt_scales{a}", align_bytes=64)

        def deal_words(a, g):
            nc.vector.tensor_copy(
                out=dealt_words[a, g][:].rearrange("p (t m b) -> p t m b", t=2, b=2),
                in_=w_words[a][:].rearrange("p (m t b) -> p t m b", t=PACK, b=2)[:, 2 * g : 2 * g + 2],
            )

        def deal_scales(a, g):
            nc.vector.tensor_copy(
                out=dealt_scales[a, g][:].rearrange("p (t m) -> p t m", t=2),
                in_=w_scales[a][:].rearrange("p (m t) -> p t m", t=PACK)[:, 2 * g : 2 * g + 2],
            )

        for a in (BW, RT):
            open_dealt(a, 0)

        picked_words = [keep.tile([P, HALF], U32, name=f"picked_words{h}", align_bytes=64) for h in range(2)]
        picked_scales = [keep.tile([P, HALF], U8, name=f"picked_scales{h}", align_bytes=64) for h in range(2)]

        def pick_scales(h):
            nc.vector.tensor_copy(out=picked_scales[h][:], in_=x_scale_table[:].indirect(offs_sb[:, list_halves[h]]))

        def pick_words(h):
            nc.vector.tensor_copy(out=picked_words[h][:], in_=x_word_table[:].indirect(offs_sb[:, list_halves[h]]))

        soft = [keep.tile([P, 2, S], F32, name=f"soft{t}") for t in range(PACK)]
        btl = [keep.tile([P, S], F32, name=f"btl{t}") for t in range(PACK)]
        bdp = [keep.tile([P, S], F32, name=f"bdp{t}") for t in range(PACK)]
        cross = [keep.tile([P, S], F32, name=f"cross{t}") for t in range(PACK)]
        den = [keep.tile([P, S], F32, name=f"den{t}") for t in range(PACK)]
        que_half = keep.tile([P, S], F32, name="que_half")
        pairsum = [keep.tile([P, S // 2], F32, name=f"pairsum{t}") for t in range(PACK)]
        log_pairsum = keep.tile([P, PACK, S // 2], F32, name="log_pairsum")
        top = keep.tile([P, PACK, S], F32, name="top")
        banks = {}

        def product(t, a, h, slot):
            banks[t, a, h] = psum.tile([P, HALF], F32, name=f"acc{t}_{a}_{h}", tag=f"bank{slot}_{a}_{h}")
            g, i = divmod(t, 2)
            nc.tensor.matmul_mx(
                out=banks[t, a, h][:],
                lhsT=dealt_words[a, g][:, 2 * P * i : 2 * P * (i + 1)].bitcast(FP4X4),
                lhsT_scale=dealt_scales[a, g][:, P * i : P * (i + 1)],
                rhs=picked_words[h][:].bitcast(FP8X4),
                rhs_scale=picked_scales[h][:],
                start=True,
                stop=True,
            )

        def sigmoid(t, a, h):
            nc.scalar.activation(out=soft[t][:, a, halves[h]], in_=banks[t, a, h][:], func=ACT.Sigmoid, scale=-1.0)

        def log_pieces(t):
            return LOG_PIECES_FIRST if t % 2 == 0 else LOG_PIECES_SECOND

        def logs(t):
            for lo, hi in log_pieces(t):
                nc.scalar.activation(out=soft[t][:, :, lo:hi], in_=soft[t][:, :, lo:hi], func=ACT.Ln, bias=TINY)

        def softplus(t):
            for lo, hi in log_pieces(t):
                h = lo // HALF
                for a, dst in ((RT, soft[t][:, RT, lo:hi]), (BW, btl[t][:, lo:hi])):
                    nc.vector.scalar_tensor_tensor(
                        out=dst, in0=soft[t][:, a, lo:hi], scalar=-1.0,
                        in1=banks[t, a, h][:, lo - h * HALF : hi - h * HALF], op0=ALU.mult, op1=ALU.max,
                    )

        def overflow(t):
            for c in halves:
                nc.vector.scalar_tensor_tensor(
                    out=bdp[t][:, c], in0=soft[t][:, RT, c], scalar=0.3, in1=btl[t][:, c], op0=ALU.add, op1=ALU.mult
                )
            for c in halves:
                nc.vector.scalar_tensor_tensor(
                    out=over[t][:, c], in0=bdp[t][:, c], scalar=-0.7, in1=over[t][:, c], op0=ALU.mult, op1=ALU.add
                )

        def share(dst, window):
            for h in range(2):
                nc.scalar.activation(
                    out=dst[:, halves[h]], in_=window[:].indirect(shr_sb[:, list_halves[h]]), func=ACT.Copy, bias=0.5
                )

        def denominator(t):
            for c in halves:
                nc.vector.scalar_tensor_tensor(
                    out=den[t][:, c], in0=over[t][:, c], scalar=0.0, in1=den[t][:, c], op0=ALU.max, op1=ALU.add
                )

        def denominator_with_gather(t):
            for c in halves:
                nc.vector.tensor_scalar(
                    out=que_half[:, c], in0=over[t][:, c], scalar1=0.0, scalar2=0.5, op0=ALU.max, op1=ALU.add
                )
            for h in range(2):
                nc.vector.tensor_tensor(
                    out=den[t][:, halves[h]], in0=btl[t][:].indirect(shr_sb[:, list_halves[h]]),
                    in1=que_half[:, halves[h]], op=ALU.add,
                )

        def by_pairs(ap):
            return ap.rearrange("p (v d) -> p v d", d=2)

        def pair_sums(t):
            for c in halves:
                nc.vector.scalar_tensor_tensor(
                    out=by_pairs(cross[t][:, c]), in0=by_pairs(cross[t][:, c]), scalar=0.5,
                    in1=by_pairs(den[t][:, c])[:, :, ::-1], op0=ALU.max, op1=ALU.mult,
                )
            for c in halves:
                nc.vector.tensor_tensor(out=den[t][:, c], in0=btl[t][:, c], in1=cross[t][:, c], op=ALU.mult)
            for h in range(2):
                members = by_pairs(den[t][:, halves[h]])
                nc.vector.tensor_tensor(
                    out=pairsum[t][:, h * HALF // 2 : (h + 1) * HALF // 2],
                    in0=members[:, :, 0], in1=members[:, :, 1], op=ALU.add,
                )

        def numerator(t):
            for c in halves:
                nc.vector.scalar_tensor_tensor(
                    out=top[:, t, c], in0=bdp[t][:, c], scalar=unit_sb[:, t : t + 1], in1=cross[t][:, c],
                    op0=ALU.mult, op1=ALU.mult,
                )

        hid = {}

        def hidden(k):
            lo, hi = OUT_PIECES[k]
            n = hi - lo
            inverse = keep.tile([P, n // 2, PACK], F32, name=f"inverse{k}")
            nc.scalar.activation(
                out=inverse[:], in_=log_pairsum[:, :, lo // 2 : hi // 2].rearrange("p t v -> p v t"),
                func=ACT.Exp, scale=-1.0,
            )
            hid[k] = keep.tile([P, n * PACK], BF16, name=f"hid{k}", align_bytes=64)
            nc.vector.tensor_tensor(
                out=hid[k][:].rearrange("p (v d t) -> p v t d", d=2, t=PACK),
                in0=top[:, :, lo:hi].rearrange("p t (v d) -> p v t d", d=2),
                in1=inverse[:].unsqueeze(3).to_broadcast([P, n // 2, PACK, 2]),
                op=ALU.mult,
            )

        def finish(k):
            lo, hi = OUT_PIECES[k]
            n = hi - lo
            codes = keep.tile([P, n], U32, name=f"codes{k}", align_bytes=64)
            scales = keep.tile([P, n], U8, name=f"scales{k}", align_bytes=64)
            nc.vector.quantize_mx(out=codes[:].bitcast(FP8X4), scales=scales[:], in_=hid[k][:])
            acc = psum.tile([P, n], F32, name=f"res{k}", tag=f"bank{k // 4}_{k // 2 % 2}_{k % 2}")
            nc.tensor.matmul_mx(
                out=acc[:], lhsT=w3_word_sb[:].bitcast(FP4X4), lhsT_scale=w3_scale_sb[:],
                rhs=codes[:].bitcast(FP8X4), rhs_scale=scales[:], start=True, stop=True,
            )
            res = keep.tile([P, n], F32, name=f"out{k}")
            nc.scalar.copy(out=res[:], in_=acc[:])
            nc.sync.dma_start(out=out[:, lo:hi], in_=res[:])

        for a in (BW, RT):
            deal_words(a, 0)
        for h in range(2):
            pick_scales(h)
        deal_scales(BW, 0)
        pick_words(0)
        deal_scales(RT, 0)
        pick_words(1)
        for a in (BW, RT):
            for h in range(2):
                for t in (1, 0):
                    product(t, a, h, t)
                for t in (1, 0):
                    sigmoid(t, a, h)

        for a in (BW, RT):
            open_dealt(a, 1)
            deal_words(a, 1)
            deal_scales(a, 1)

        infl_rows = infl.rearrange("(p t) j -> p t j", t=PACK)
        over = [
            keep.tile([P, S], F32, name=f"over{t}", tag=tag, align_bytes=64)
            for t, tag in enumerate(("raw0", "raw2", "raw1", "raw3"))
        ]
        for t in range(PACK):
            nc.sync.dma_start(out=over[t][:], in_=infl_rows[:, t, :])

        for t in (0, 1):
            logs(t)
        for t in (0, 1):
            softplus(t)
            overflow(t)
        share(den[0], btl[0])
        share(cross[0], over[0])

        for t, slot in ((3, 0), (2, 1)):
            for a in (BW, RT):
                for h in range(2):
                    product(t, a, h, slot)
                    sigmoid(t, a, h)

        unit_sb = keep.tile([P, PACK], F32, name="unit_sb", tag="dealt_scales0", align_bytes=64)
        w3_word_sb = keep.tile([P, 2 * N], U8, name="w3_word_sb", tag="dealt_words0", align_bytes=64)
        w3_scale_sb = keep.tile([P, N], U8, name="w3_scale_sb", tag="dealt_words1", align_bytes=64)
        nc.sync.dma_start(out=unit_sb[:], in_=unit.rearrange("(p t) o -> p (t o)", t=PACK))
        nc.sync.dma_start(out=w3_word_sb[:].bitcast(I32), in_=w3_words[0].bitcast(I32))
        nc.vector.memset(w3_scale_sb[:].bitcast(I32), 0)
        for r in range(4):
            load_scale_rows(nc.sync, w3_scale_sb, w3_scales, r)

        for t in (2, 3):
            logs(t)
        denominator(0)
        pair_sums(0)
        numerator(0)
        share(cross[VECTOR_GATHER_TILE], over[VECTOR_GATHER_TILE])
        denominator_with_gather(VECTOR_GATHER_TILE)
        for t in (2, 3):
            softplus(t)
            overflow(t)
        for t in (2, 3):
            share(den[t], btl[t])
            share(cross[t], over[t])
        for t in (1, 2, 3):
            if t != VECTOR_GATHER_TILE:
                denominator(t)
            pair_sums(t)
        for t in range(PACK):
            nc.scalar.activation(out=log_pairsum[:, t, :], in_=pairsum[t][:], func=ACT.Ln)
        for t in (1, 2, 3):
            numerator(t)

        hidden(0)
        for k in range(1, len(OUT_PIECES)):
            hidden(k)
            finish(k - 1)
        finish(len(OUT_PIECES) - 1)
